import numpy as np
import ml_dtypes


def mxq(x, axis, fmt="e4m3"):
    dtype, down = {"e4m3": (ml_dtypes.float8_e4m3fn, 7), "e5m2": (ml_dtypes.float8_e5m2, 14)}[fmt]
    v = np.moveaxis(np.asarray(x, np.float32).astype(ml_dtypes.bfloat16).astype(np.float64), axis, -1)
    blocks = v.reshape(v.shape[:-1] + (-1, 32))
    amax = np.abs(blocks).max(-1, keepdims=True)
    byte = np.maximum(np.where(amax > 0, np.frexp(amax)[1] - 1 + 127, 0) - down, 1)
    scale = np.exp2(byte - 127.0)
    codes = (blocks / scale).astype(np.float32).astype(dtype).astype(np.float64)
    return np.moveaxis((codes * scale).reshape(v.shape), -1, axis)


WIDE = False


def mx_kscale(k):
    if not WIDE:
        return np.ones(k)
    levels = np.array([24, -24, 12, -12, 0])
    if k % 512:
        return np.exp2(np.random.permutation(np.resize(levels, k // 32))).repeat(32)
    a = np.empty((k // 512, 16))
    for p in range(k // 512):
        a[p, :8] = np.random.permutation(np.resize(levels, 8))
        for g in range(8):
            far = levels[np.abs(levels - a[p, g]) >= 10]
            a[p, g + 8] = far[np.random.randint(len(far))]
    return np.exp2(a.ravel()).repeat(32)


def f64(x):
    return np.asarray(x).astype(np.float64)


def striped(idx):
    return np.tile(idx.reshape(-1, 16).T, (8, 1)).astype(np.uint16)


def unstriped(offs):
    return offs[:16].T.reshape(-1).astype(np.int64)


E2M1 = np.array([0.0, 0.5, 1.0, 1.5, 2.0, 3.0, 4.0, 6.0, -0.0, -0.5, -1.0, -1.5, -2.0, -3.0, -4.0, -6.0])


def pack_weight(w, fmt):
    k, n = w.shape
    w = f64(np.asarray(w, np.float32).astype(ml_dtypes.bfloat16)).reshape(k // 32, 32, n)
    amax = np.abs(w).max(1)
    if fmt == "e4m3":
        byte = np.frexp(amax)[1] - 1 + 127 - 7
    else:
        mant, ex = np.frexp(amax / 6.0)
        byte = np.where(mant > 0.5, ex, ex - 1) + 127
    byte = np.clip(np.where(amax > 0, byte, 1), 1, 254)
    scaled = (w * np.exp2(127.0 - byte)[:, None, :]).reshape(k, n).astype(np.float32)
    by_word = np.ascontiguousarray(scaled.reshape(k // 512, 128, 4, n).transpose(0, 1, 3, 2))
    if fmt == "e4m3":
        words = by_word.astype(ml_dtypes.float8_e4m3fn).view(np.uint8)
    else:
        c = by_word.astype(ml_dtypes.float4_e2m1fn).view(np.uint8) & 0xF
        words = (c[..., 0::2] | (c[..., 1::2] << 4)).reshape(k // 512, 128, 2 * n)
    return np.ascontiguousarray(words), np.ascontiguousarray(byte.astype(np.uint8).reshape(k // 512, 16, n))


def unpack_weight(words, scales, fmt):
    g, _, n = scales.shape
    words = np.ascontiguousarray(words).reshape(g, 128, n, -1)
    if fmt == "e4m3":
        vals = words.view(ml_dtypes.float8_e4m3fn).astype(np.float64)
    else:
        nib = np.empty((g, 128, n, 4), np.uint8)
        nib[..., 0::2] = words & 0xF
        nib[..., 1::2] = words >> 4
        vals = E2M1[nib]
    vals = vals * np.repeat(np.exp2(scales.astype(np.float64) - 127.0), 8, axis=1)[..., None]
    return vals.transpose(0, 1, 3, 2).reshape(g * 512, n)


def pack_table4(v):
    words, scales = pack_weight(v, "e2m1")
    g, t = words.shape[0] // 2, v.shape[1]
    return np.ascontiguousarray(words.reshape(g, 2, 128, t, 2).transpose(0, 2, 3, 1, 4).reshape(g, 128, t, 4)), scales


def unpack_table4(words, scales):
    g, _, t, _ = words.shape
    return unpack_weight(words.reshape(g, 128, t, 2, 2).transpose(0, 3, 1, 2, 4).reshape(2 * g, 128, 2 * t), scales, "e2m1")


K, R, N, T, J = 1024, 1024, 512, 4096, 1024


def setup_inputs():
    n = np.random.standard_normal
    s = mx_kscale(K)[:, None]
    u = mx_kscale(R)[:, None]
    p_tab = pack_table4(n((K, T)) * s)
    p_w0 = pack_weight(n((K, R)) / np.sqrt(3 * K) / s * u.T, "e2m1")
    p_w1 = pack_weight(n((K, R)) / np.sqrt(3 * K) / s * u.T, "e4m3")
    p_wd = pack_weight(n((R, N)) / np.sqrt(R) / u, "e4m3")
    return {
        "tab_words": p_tab[0],
        "tab_scales": p_tab[1],
        "w0_words": p_w0[0],
        "w0_scales": p_w0[1],
        "w1_words": p_w1[0],
        "w1_scales": p_w1[1],
        "w2": (n((K, R)) / np.sqrt(3 * K) / s * u.T).astype(np.float32),
        "wd_words": p_wd[0],
        "wd_scales": p_wd[1],
        "res": (n((N, J))).astype(np.float32),
        "offs": striped(np.concatenate([np.random.permutation(T)[:J] for _ in range(3)])),
    }


def reference(tab_words, tab_scales, w0_words, w0_scales, w1_words, w1_scales, w2, wd_words, wd_scales, res, offs):
    idx = unstriped(offs).reshape(3, J)
    tab_ = unpack_table4(tab_words, tab_scales)[:, idx]
    w0_ = unpack_weight(w0_words, w0_scales, "e2m1")
    w1_ = unpack_weight(w1_words, w1_scales, "e4m3")
    w2_ = mxq(f64(w2), 0, "e4m3")
    a = w0_.T @ tab_[:, 0] + w1_.T @ tab_[:, 1] + w2_.T @ tab_[:, 2]
    h = np.maximum(a, 0.0)
    h_ = mxq(h, 0, "e4m3")
    wd_ = unpack_weight(wd_words, wd_scales, "e4m3")
    y = wd_.T @ h_
    return f64(res) + y

@@ -1,0 +1,305 @@
+from contextlib import ExitStack
+
+import concourse.mybir as mybir
+
+K, R, N, T, J = 1024, 1024, 512, 4096, 1024
+FLOPS = 2 * (3 * K * R * J + R * N * J)
+
+F32 = mybir.dt.float32
+BF16 = mybir.dt.bfloat16
+I32 = mybir.dt.int32
+U32 = mybir.dt.uint32
+U16 = mybir.dt.uint16
+U8 = mybir.dt.uint8
+FP8X4 = mybir.dt.float8_e4m3fn_x4
+FP4X4 = mybir.dt.float4_e2m1fn_x4
+RELU = mybir.ActivationFunctionType.Relu
+ADD = mybir.AluOpType.add
+
+P = 128
+W = 512
+
+
+def tile_list_rvq_relu_res_kernel(
+    tc, tab_words, tab_scales, w0_words, w0_scales, w1_words, w1_scales, w2, wd_words, wd_scales, res, offs, out
+):
+    nc = tc.nc
+    with ExitStack() as ctx:
+        keep = ctx.enter_context(tc.tile_pool(name="keep", bufs=1))
+        psum = ctx.enter_context(tc.psum_pool(name="psum", bufs=8))
+
+        def held(shape, dtype, name, tag=None):
+            return keep.tile(shape, dtype, name=name, tag=tag or name, align_bytes=64)
+
+        offsets = keep.tile([P, 3 * J // 16], U16, name="offsets")
+        nc.sync.dma_start(offsets[:], offs)
+
+        raw_sc = [held([P, R], U8, "w0_sc_raw", "slot0"), held([P, R], U8, "w1_sc_raw")]
+        up_sc = [held([P, R], U8, "w0_sc_up"), held([P, R], U8, "w1_sc_up")]
+        tab_up = held([P, 6, W], U8, "tab_up")
+        for t_ in (raw_sc[0], raw_sc[1], up_sc[0], up_sc[1]):
+            nc.vector.memset(t_[:].bitcast(I32), 0)
+        nc.vector.memset(tab_up[:].rearrange("p a w -> p (a w)").bitcast(I32), 0)
+
+        warm = held([P, 16], BF16, "warm")
+        nc.scalar.activation(warm[:], up_sc[0][:, 0:32].bitcast(BF16), RELU)
+
+        tsc = held([P, T], U8, "tsc")
+        rows = tab_scales.rearrange("a q t -> (a q) t").bitcast(I32)
+        for q in range(4):
+            for h in range(2):
+                nc.sync.dma_start(
+                    tsc[32 * q + 16 * h : 32 * q + 16 * h + 16, :].bitcast(I32),
+                    rows[4 * q + 4 * h : 4 * q + 4 * h + 16, :],
+                )
+
+        def load_scales(eng, tile_, src):
+            for q in range(4):
+                eng.dma_start(tile_[32 * q : 32 * q + 8, :].bitcast(I32), src[:, 4 * q : 4 * q + 4, :].bitcast(I32))
+
+        load_scales(nc.sync, raw_sc[0], w0_scales)
+        tw = held([P, T], I32, "tw")
+        w0_raw = [held([P, 2, W // 2], I32, "w0_raw%d" % b, ("w0_raw0", "slot2")[b]) for b in range(2)]
+        w1_raw = [held([P, 2, W], I32, "w1_raw%d" % b, ("w1_raw0", "slot4")[b]) for b in range(2)]
+        w2_raw = {}
+        for b in range(2):
+            nc.sync.dma_start(w0_raw[b][:], w0_words.rearrange("a p c -> p a c")[:, :, 2 * W * b : 2 * W * (b + 1)].bitcast(I32))
+            if b == 0:
+                nc.sync.dma_start(tw[:], tab_words[0].rearrange("p t i -> p (t i)").bitcast(I32))
+        load_scales(nc.sync, raw_sc[1], w1_scales)
+        for b in range(2):
+            nc.sync.dma_start(
+                w1_raw[b][:], w1_words.rearrange("a p r i -> p a (r i)")[:, :, 4 * W * b : 4 * W * (b + 1)].bitcast(I32)
+            )
+        late = {}
+
+        def load_w2(b, a):
+            w2_raw[b, a] = held([P, 4, W], F32, "w2_raw%d%d" % (b, a), "slot%d" % (2 * b + a))
+            nc.sync.dma_start(w2_raw[b, a][:], w2[W * a : W * (a + 1), W * b : W * (b + 1)].rearrange("(p i) c -> p i c", i=4))
+
+        def load_wd():
+            late["wd"] = held([P, 2, N], I32, "wd", "slot4")
+            late["wd_sc"] = held([P, N], U8, "wd_sc", "w1_sc_raw")
+            nc.vector.memset(late["wd_sc"][:].bitcast(I32), 0)
+            load_scales(nc.sync, late["wd_sc"], wd_scales)
+            nc.sync.dma_start(late["wd"][:], wd_words.rearrange("a p n i -> p a (n i)").bitcast(I32))
+
+        res_sb = {}
+
+        def load_res(c):
+            res_sb[c] = held([P, 4, W], F32, "res%d" % c, "slot%d" % (2 * c + 1))
+            nc.sync.dma_start(res_sb[c][:], res[:, W * c : W * (c + 1)].rearrange("(u p) j -> p u j", p=P))
+
+        tab_lo = {}
+        tab_x = {}
+        w_lo = {}
+        w_x = {}
+        w2_sc = {}
+        h_x = {}
+        h_sc = {}
+        banks = {}
+
+        def piece(g, c):
+            k0 = (g * J + c * W) // 16
+            return offsets[:, k0 : k0 + W // 16]
+
+        def gather_scales(g, c):
+            tab_lo[g, c] = held([P, W], U8, "tab_lo%d%d" % (g, c), {(0, 1): "w0_raw0", (1, 1): "w1_raw0", (2, 1): "both20"}.get((g, c)))
+            nc.vector.tensor_copy(tab_lo[g, c][:], tsc[:].indirect(piece(g, c)))
+            (nc.scalar if c == 0 else nc.sync).dma_start(tab_up[0:100, 2 * g + c, :].bitcast(I32), tab_lo[g, c][28:128, :].bitcast(I32))
+
+        def gather_words(g, c):
+            both = held([P, W], U32, "both%d%d" % (g, c), {(0, 0): "slot1", (1, 0): "slot3"}.get((g, c)))
+            nc.vector.tensor_copy(both[:], tw[:].bitcast(U32).indirect(piece(g, c)))
+            tab_x[g, c] = held([P, 2, 2 * W], U8, "tab_x%d%d" % (g, c))
+            nc.vector.tensor_copy(tab_x[g, c][:].bitcast(U16), both[:].bitcast(U16).rearrange("p (j d) -> p d j", d=2))
+
+        def order_scales(g):
+            w_lo[g] = held([P, R], U8, "w_lo%d" % g)
+            nc.vector.tensor_copy(
+                w_lo[g][:].rearrange("p (b t m) -> p b t m", b=2, t=4), raw_sc[g][:].rearrange("p (b m t) -> p b t m", b=2, t=4)
+            )
+            nc.scalar.dma_start(up_sc[g][0:100, :].bitcast(I32), w_lo[g][4:104, :].bitcast(I32))
+
+        def order_w0(b):
+            w_x[0, b] = held([P, 2, 2 * W], U8, "w0_x%d" % b)
+            nc.vector.tensor_copy(
+                w_x[0, b][:].bitcast(U16).rearrange("p a (t m) -> p a t m", t=4),
+                w0_raw[b][:].bitcast(U16).rearrange("p a (m t) -> p a t m", t=4),
+            )
+
+        def order_w1(b):
+            w_x[1, b] = held([P, 2, W], I32, "w1_x%d" % b)
+            nc.vector.tensor_copy(
+                w_x[1, b][:].rearrange("p a (t m) -> p a m t", t=4), w1_raw[b][:].rearrange("p a (m t) -> p a m t", t=4)
+            )
+
+        w2_bf = {}
+
+        def cast_w2(b, a):
+            w2_bf[b, a] = held([P, 4 * W], BF16, "w2_bf%d%d" % (b, a))
+            nc.scalar.copy(
+                w2_bf[b, a][:].rearrange("p (t m i) -> p m i t", t=4, i=4),
+                w2_raw[b, a][:].rearrange("p i (m t) -> p m i t", t=4),
+            )
+
+        def quant_w2(b, a):
+            w_x[2, b, a] = held([P, W], U32, "w2_x%d%d" % (b, a))
+            w2_sc[b, a] = held([P, W], U8, "w2_sc%d%d" % (b, a))
+            nc.vector.quantize_mx(out=w_x[2, b, a][:].bitcast(FP8X4), scales=w2_sc[b, a][:], in_=w2_bf[b, a][:])
+
+        def mm1(dst, g, a, b, t, c, j0, n):
+            m = slice(P * t, P * (t + 1))
+            if g == 0:
+                lhs = w_x[0, b][:, a, 2 * P * t : 2 * P * (t + 1)].bitcast(FP4X4)
+            elif g == 1:
+                lhs = w_x[1, b][:, a, m].bitcast(FP8X4)
+            else:
+                lhs = w_x[2, b, a][:, m].bitcast(FP8X4)
+            if g < 2:
+                lhs_sc = (w_lo, up_sc)[a][g][:, W * b + P * t : W * b + P * (t + 1)]
+            else:
+                lhs_sc = w2_sc[b, a][:, m]
+            rhs_sc = tab_lo[g, c][:, j0 : j0 + n] if a == 0 else tab_up[:, 2 * g + c, j0 : j0 + n]
+            nc.tensor.matmul_mx(
+                out=dst,
+                lhsT=lhs,
+                lhsT_scale=lhs_sc,
+                rhs=tab_x[g, c][:, a, 2 * j0 : 2 * (j0 + n)].bitcast(FP4X4),
+                rhs_scale=rhs_sc,
+                start=(g == 0 and a == 0),
+                stop=(g == 2 and a == 1),
+            )
+
+        def wide(g, b, c):
+            if g == 0:
+                banks[b, c] = [psum.tile([P, W], F32, name="bank") for t in range(4)]
+            if g < 2:
+                order = [(a, t) for a in range(2) for t in range(4)]
+            else:
+                order = [(0, t) for t in range(2)] + [(1, 0), (0, 2), (1, 1), (0, 3), (1, 2), (1, 3)]
+            for a, t in order:
+                mm1(banks[b, c][t][:], g, a, b, t, c, 0, W)
+
+        planes = {}
+
+        def drain(b, c):
+            planes[b, c] = held([P, 4, W], BF16, "h_pl%d%d" % (b, c))
+            for t in range(4):
+                nc.scalar.activation(planes[b, c][:, t, :], banks[b, c][t][:], RELU)
+
+        woven = {}
+
+        def weave(b, c):
+            woven[b, c] = held([P, 4 * W], BF16, "h_wv%d%d" % (b, c))
+            nc.vector.tensor_copy(
+                woven[b, c][:].rearrange("p (c i t) -> p c t i", i=4, t=4),
+                planes[b, c][:].rearrange("p t (c i) -> p c t i", i=4),
+            )
+
+        def quant_h(b, c):
+            h_x[b, c] = held([P, W], U32, "h_x%d%d" % (b, c))
+            h_sc[b, c] = held([P, W], U8, "h_sc%d%d" % (b, c))
+            nc.vector.quantize_mx(out=h_x[b, c][:].bitcast(FP8X4), scales=h_sc[b, c][:], in_=woven[b, c][:])
+
+        def mm2(dst, u, b, x, sc):
+            nc.tensor.matmul_mx(
+                out=dst,
+                lhsT=late["wd"][:, b, P * u : P * (u + 1)].bitcast(FP8X4),
+                lhsT_scale=late["wd_sc"][4 * b :, P * u : P * (u + 1)],
+                rhs=x.bitcast(FP8X4),
+                rhs_scale=sc,
+                start=(b == 0),
+                stop=(b == 1),
+            )
+
+        def second_wide(u):
+            bank = psum.tile([P, W], F32, name="bank")
+            for b in range(2):
+                mm2(bank[:], u, b, h_x[b, 0][:], h_sc[b, 0][:])
+            o = held([P, W], F32, "o_wide%d" % u)
+            nc.vector.tensor_tensor(o[:], bank[:], res_sb[0][:, u, :], ADD)
+            nc.sync.dma_start(out[P * u : P * (u + 1), 0:W], o[:])
+
+        def narrow(s):
+            bank = psum.tile([P, W], F32, name="bank")
+            for t in range(4):
+                for g in range(3):
+                    for a in range(2):
+                        mm1(bank[:, P * t : P * (t + 1)], g, a, 1, t, 1, P * s, P)
+            wv = held([P, W], BF16, "h_nw%d" % s)
+            nc.scalar.activation(
+                wv[:].rearrange("p (j t) -> p j t", t=4), bank[:].rearrange("p (t j) -> p j t", t=4), RELU
+            )
+            h_x[1, 1, s] = held([P, P], U32, "h_nx%d" % s)
+            h_sc[1, 1, s] = held([P, P], U8, "h_nsc%d" % s)
+            nc.vector.quantize_mx(out=h_x[1, 1, s][:].bitcast(FP8X4), scales=h_sc[1, 1, s][:], in_=wv[:])
+
+        def second_narrow(s):
+            bank = psum.tile([P, W], F32, name="bank")
+            js = slice(P * s, P * (s + 1))
+            for u in range(4):
+                mm2(bank[:, P * u : P * (u + 1)], u, 0, h_x[0, 1][:, js], h_sc[0, 1][:, js])
+                mm2(bank[:, P * u : P * (u + 1)], u, 1, h_x[1, 1, s][:], h_sc[1, 1, s][:])
+            o = held([P, 4, P], F32, "o_nw%d" % s)
+            nc.vector.tensor_tensor(o[:], bank[:].rearrange("p (u j) -> p u j", u=4), res_sb[1][:, :, js], ADD)
+            nc.sync.dma_start(out[:, W + P * s : W + P * (s + 1)].rearrange("(u p) j -> p u j", p=P), o[:])
+
+        gather_scales(0, 0)
+        order_scales(0)
+        load_w2(0, 0)
+        gather_words(0, 0)
+        load_w2(0, 1)
+        order_w0(0)
+        order_w0(1)
+        load_w2(1, 0)
+        wide(0, 0, 0)
+        wide(0, 1, 0)
+        gather_scales(1, 0)
+        order_scales(1)
+        gather_words(1, 0)
+        load_w2(1, 1)
+        order_w1(0)
+        order_w1(1)
+        load_wd()
+        gather_scales(2, 0)
+        wide(1, 0, 0)
+        wide(1, 1, 0)
+        gather_words(2, 0)
+        cast_w2(0, 0)
+        cast_w2(0, 1)
+        load_res(0)
+        quant_w2(0, 0)
+        quant_w2(0, 1)
+        wide(2, 0, 0)
+        gather_scales(0, 1)
+        gather_words(0, 1)
+        cast_w2(1, 0)
+        drain(0, 0)
+        cast_w2(1, 1)
+        load_res(1)
+        wide(0, 0, 1)
+        quant_w2(1, 0)
+        quant_w2(1, 1)
+        gather_scales(1, 1)
+        gather_words(1, 1)
+        wide(2, 1, 0)
+        drain(1, 0)
+        gather_scales(2, 1)
+        gather_words(2, 1)
+        wide(1, 0, 1)
+        wide(2, 0, 1)
+        drain(0, 1)
+        weave(0, 0)
+        weave(1, 0)
+        quant_h(0, 0)
+        quant_h(1, 0)
+        narrow(0)
+        weave(0, 1)
+        quant_h(0, 1)
+        for u in range(4):
+            second_wide(u)
+        for s in range(1, 4):
+            narrow(s)
+            second_narrow(s - 1)
+        second_narrow(3)

@@ -16,6 +16,22 @@ FP4X4 = mybir.dt.float4_e2m1fn_x4
 RELU = mybir.ActivationFunctionType.Relu
 ADD = mybir.AluOpType.add
 
+REUSES = {
+    "w1_sc_raw": "w0_raw0",
+    "wd_sc": "w0_raw0",
+    "both10": "w0_raw1",
+    "both20": "w1_raw0",
+    "tab_lo01": "w1_raw1",
+    "both01": "w2_bf01",
+    "both11": "w2_bf11",
+    "tab_lo21": "w2_bf10",
+    "both21": "w2_bf11",
+    "h_wv10": "w2_bf01",
+    "res0": "both10",
+    "h_wv00": "w2_bf11",
+    "h_pl10": "both21",
+    "res1": "w2_raw111"
+}
 P = 128
 W = 512
 
@@ -28,68 +44,93 @@ def tile_list_rvq_relu_res_kernel(
         keep = ctx.enter_context(tc.tile_pool(name="keep", bufs=1))
         psum = ctx.enter_context(tc.psum_pool(name="psum", bufs=8))
 
-        def held(shape, dtype, name, tag=None):
-            return keep.tile(shape, dtype, name=name, tag=tag or name, align_bytes=64)
+        def held(shape, dtype, name):
+            return keep.tile(shape, dtype, name=name, tag=REUSES.get(name, name), align_bytes=64)
 
         offsets = keep.tile([P, 3 * J // 16], U16, name="offsets")
         nc.sync.dma_start(offsets[:], offs)
 
-        raw_sc = [held([P, R], U8, "w0_sc_raw", "slot0"), held([P, R], U8, "w1_sc_raw")]
+        raw_sc = {0: held([P, R], U8, "w0_sc_raw")}
         up_sc = [held([P, R], U8, "w0_sc_up"), held([P, R], U8, "w1_sc_up")]
         tab_up = held([P, 6, W], U8, "tab_up")
-        for t_ in (raw_sc[0], raw_sc[1], up_sc[0], up_sc[1]):
+        tsc = held([P, T], U8, "tsc")
+        nc.vector.memset(tsc[:, 0 : T // 2].bitcast(I32), 0)
+        nc.gpsimd.memset(tsc[:, T // 2 : T].bitcast(I32), 0)
+        for t_ in (raw_sc[0], up_sc[0], up_sc[1]):
             nc.vector.memset(t_[:].bitcast(I32), 0)
         nc.vector.memset(tab_up[:].rearrange("p a w -> p (a w)").bitcast(I32), 0)
 
-        warm = held([P, 16], BF16, "warm")
-        nc.scalar.activation(warm[:], up_sc[0][:, 0:32].bitcast(BF16), RELU)
 
-        tsc = held([P, T], U8, "tsc")
-        rows = tab_scales.rearrange("a q t -> (a q) t").bitcast(I32)
-        for q in range(4):
-            for h in range(2):
-                nc.sync.dma_start(
-                    tsc[32 * q + 16 * h : 32 * q + 16 * h + 16, :].bitcast(I32),
-                    rows[4 * q + 4 * h : 4 * q + 4 * h + 16, :],
-                )
+        def warm_up():
+            warm = held([P, 16], BF16, "warm")
+            nc.scalar.activation(warm[:], up_sc[0][:, 0:32].bitcast(BF16), RELU)
 
-        def load_scales(eng, tile_, src):
-            for q in range(4):
-                eng.dma_start(tile_[32 * q : 32 * q + 8, :].bitcast(I32), src[:, 4 * q : 4 * q + 4, :].bitcast(I32))
 
-        load_scales(nc.sync, raw_sc[0], w0_scales)
-        tw = held([P, T], I32, "tw")
-        w0_raw = [held([P, 2, W // 2], I32, "w0_raw%d" % b, ("w0_raw0", "slot2")[b]) for b in range(2)]
-        w1_raw = [held([P, 2, W], I32, "w1_raw%d" % b, ("w1_raw0", "slot4")[b]) for b in range(2)]
+        def load_scales(eng, tile_, src, which=range(4)):
+            rows = src.rearrange("a (q r) t -> r q a t", r=4)
+            for r in which:
+                eng.dma_start(tile_[r:P:16, :].bitcast(I32), rows[r].bitcast(I32))
+
+        w0_raw = {}
+        w1_raw = {}
         w2_raw = {}
-        for b in range(2):
-            nc.sync.dma_start(w0_raw[b][:], w0_words.rearrange("a p c -> p a c")[:, :, 2 * W * b : 2 * W * (b + 1)].bitcast(I32))
-            if b == 0:
-                nc.sync.dma_start(tw[:], tab_words[0].rearrange("p t i -> p (t i)").bitcast(I32))
-        load_scales(nc.sync, raw_sc[1], w1_scales)
-        for b in range(2):
+        late = {}
+        res_sb = {}
+
+        def load_w0(b, eng=nc.sync):
+            w0_raw[b] = held([P, 2, W // 2], I32, "w0_raw%d" % b)
+            eng.dma_start(w0_raw[b][:], w0_words.rearrange("a p c -> p a c")[:, :, 2 * W * b : 2 * W * (b + 1)].bitcast(I32))
+
+        def load_w1(b):
+            w1_raw[b] = held([P, 2, W], I32, "w1_raw%d" % b)
             nc.sync.dma_start(
                 w1_raw[b][:], w1_words.rearrange("a p r i -> p a (r i)")[:, :, 4 * W * b : 4 * W * (b + 1)].bitcast(I32)
             )
-        late = {}
 
-        def load_w2(b, a):
-            w2_raw[b, a] = held([P, 4, W], F32, "w2_raw%d%d" % (b, a), "slot%d" % (2 * b + a))
-            nc.sync.dma_start(w2_raw[b, a][:], w2[W * a : W * (a + 1), W * b : W * (b + 1)].rearrange("(p i) c -> p i c", i=4))
+        def load_w1_scales():
+            raw_sc[1] = held([P, R], U8, "w1_sc_raw")
+            nc.vector.memset(raw_sc[1][:].bitcast(I32), 0)
+            load_scales(nc.scalar, raw_sc[1], w1_scales)
+
+        def load_w2(b, a, h):
+            w2_raw[b, a, h] = held([P, 4, W // 2], F32, "w2_raw%d%d%d" % (b, a, h))
+            c0 = W * b + W // 2 * h
+            nc.sync.dma_start(w2_raw[b, a, h][:], w2[W * a : W * (a + 1), c0 : c0 + W // 2].rearrange("(p i) c -> p i c", i=4))
 
         def load_wd():
-            late["wd"] = held([P, 2, N], I32, "wd", "slot4")
-            late["wd_sc"] = held([P, N], U8, "wd_sc", "w1_sc_raw")
+            late["wd"] = held([P, 2, N], I32, "wd")
+            late["wd_sc"] = held([P, N], U8, "wd_sc")
             nc.vector.memset(late["wd_sc"][:].bitcast(I32), 0)
-            load_scales(nc.sync, late["wd_sc"], wd_scales)
+            for q in range(4):
+                nc.sync.dma_start(late["wd_sc"][32 * q : 32 * q + 8, :].bitcast(I32), wd_scales[:, 4 * q : 4 * q + 4, :].bitcast(I32))
             nc.sync.dma_start(late["wd"][:], wd_words.rearrange("a p n i -> p a (n i)").bitcast(I32))
 
-        res_sb = {}
-
         def load_res(c):
-            res_sb[c] = held([P, 4, W], F32, "res%d" % c, "slot%d" % (2 * c + 1))
+            res_sb[c] = held([P, 4, W], F32, "res%d" % c)
             nc.sync.dma_start(res_sb[c][:], res[:, W * c : W * (c + 1)].rearrange("(u p) j -> p u j", p=P))
 
+        tw = held([P, T], I32, "tw")
+
+        def load_tw(eng):
+            eng.dma_start(tw[:], tab_words[0].rearrange("p t i -> p (t i)").bitcast(I32))
+
+        load_scales(nc.scalar, tsc, tab_scales, (2, 3))
+        load_scales(nc.scalar, raw_sc[0], w0_scales)
+        warm_up()
+        load_scales(nc.sync, tsc, tab_scales, (0, 1))
+        load_w0(0)
+        load_tw(nc.sync)
+        load_w2(0, 0, 0)
+        load_w0(1)
+        load_w1(0)
+        load_w2(0, 1, 0)
+        load_w2(1, 0, 0)
+        load_w2(0, 0, 1)
+        load_w1(1)
+        load_w2(0, 1, 1)
+        load_w2(1, 0, 1)
+        load_w2(1, 1, 0)
+        load_w2(1, 1, 1)
         tab_lo = {}
         tab_x = {}
         w_lo = {}
@@ -103,23 +144,39 @@ def tile_list_rvq_relu_res_kernel(
             k0 = (g * J + c * W) // 16
             return offsets[:, k0 : k0 + W // 16]
 
+        first_lo = held([P, 3, W], U8, "first_lo")
+
         def gather_scales(g, c):
-            tab_lo[g, c] = held([P, W], U8, "tab_lo%d%d" % (g, c), {(0, 1): "w0_raw0", (1, 1): "w1_raw0", (2, 1): "both20"}.get((g, c)))
-            nc.vector.tensor_copy(tab_lo[g, c][:], tsc[:].indirect(piece(g, c)))
-            (nc.scalar if c == 0 else nc.sync).dma_start(tab_up[0:100, 2 * g + c, :].bitcast(I32), tab_lo[g, c][28:128, :].bitcast(I32))
+            if c == 0:
+                tab_lo[g, c] = first_lo[:, g, :]
+            else:
+                tab_lo[g, c] = held([P, W], U8, "tab_lo%d%d" % (g, c))[:]
+            nc.vector.tensor_copy(tab_lo[g, c], tsc[:].indirect(piece(g, c)))
+            if c == 1:
+                nc.sync.dma_start(tab_up[0:112, 3 + g, :].bitcast(I32), tab_lo[g, c][16:128, :].bitcast(I32))
+            elif g == 2:
+                nc.scalar.dma_start(
+                    tab_up[0:112, 0:3, :].rearrange("p g w -> p (g w)").bitcast(I32),
+                    first_lo[16:128].rearrange("p g w -> p (g w)").bitcast(I32),
+                )
 
         def gather_words(g, c):
-            both = held([P, W], U32, "both%d%d" % (g, c), {(0, 0): "slot1", (1, 0): "slot3"}.get((g, c)))
+            both = held([P, W], U32, "both%d%d" % (g, c))
             nc.vector.tensor_copy(both[:], tw[:].bitcast(U32).indirect(piece(g, c)))
             tab_x[g, c] = held([P, 2, 2 * W], U8, "tab_x%d%d" % (g, c))
-            nc.vector.tensor_copy(tab_x[g, c][:].bitcast(U16), both[:].bitcast(U16).rearrange("p (j d) -> p d j", d=2))
+            halves = both[:].bitcast(U16).rearrange("p (j d) -> p d j", d=2)
+            if (g, c) == (0, 0):
+                for a in range(2):
+                    nc.vector.tensor_copy(tab_x[g, c][:, a, :].bitcast(U16), halves[:, a, :])
+            else:
+                nc.vector.tensor_copy(tab_x[g, c][:].bitcast(U16), halves)
 
         def order_scales(g):
             w_lo[g] = held([P, R], U8, "w_lo%d" % g)
             nc.vector.tensor_copy(
                 w_lo[g][:].rearrange("p (b t m) -> p b t m", b=2, t=4), raw_sc[g][:].rearrange("p (b m t) -> p b t m", b=2, t=4)
             )
-            nc.scalar.dma_start(up_sc[g][0:100, :].bitcast(I32), w_lo[g][4:104, :].bitcast(I32))
+            nc.scalar.dma_start(up_sc[g][0:112, :].bitcast(I32), w_lo[g][16:128, :].bitcast(I32))
 
         def order_w0(b):
             w_x[0, b] = held([P, 2, 2 * W], U8, "w0_x%d" % b)
@@ -138,10 +195,11 @@ def tile_list_rvq_relu_res_kernel(
 
         def cast_w2(b, a):
             w2_bf[b, a] = held([P, 4 * W], BF16, "w2_bf%d%d" % (b, a))
-            nc.scalar.copy(
-                w2_bf[b, a][:].rearrange("p (t m i) -> p m i t", t=4, i=4),
-                w2_raw[b, a][:].rearrange("p i (m t) -> p m i t", t=4),
-            )
+            for h in range(2):
+                nc.scalar.copy(
+                    w2_bf[b, a][:].rearrange("p (t m i) -> p m i t", t=4, i=4)[:, 64 * h : 64 * (h + 1)],
+                    w2_raw[b, a, h][:].rearrange("p i (m t) -> p m i t", t=4),
+                )
 
         def quant_w2(b, a):
             w_x[2, b, a] = held([P, W], U32, "w2_x%d%d" % (b, a))
@@ -160,7 +218,7 @@ def tile_list_rvq_relu_res_kernel(
                 lhs_sc = (w_lo, up_sc)[a][g][:, W * b + P * t : W * b + P * (t + 1)]
             else:
                 lhs_sc = w2_sc[b, a][:, m]
-            rhs_sc = tab_lo[g, c][:, j0 : j0 + n] if a == 0 else tab_up[:, 2 * g + c, j0 : j0 + n]
+            rhs_sc = tab_lo[g, c][:, j0 : j0 + n] if a == 0 else tab_up[:, g + 3 * c, j0 : j0 + n]
             nc.tensor.matmul_mx(
                 out=dst,
                 lhsT=lhs,
@@ -190,9 +248,9 @@ def tile_list_rvq_relu_res_kernel(
 
         woven = {}
 
-        def weave(b, c):
+        def weave(b, c, copy=nc.vector.tensor_copy):
             woven[b, c] = held([P, 4 * W], BF16, "h_wv%d%d" % (b, c))
-            nc.vector.tensor_copy(
+            copy(
                 woven[b, c][:].rearrange("p (c i t) -> p c t i", i=4, t=4),
                 planes[b, c][:].rearrange("p t (c i) -> p c t i", i=4),
             )
@@ -245,61 +303,63 @@ def tile_list_rvq_relu_res_kernel(
             nc.vector.tensor_tensor(o[:], bank[:].rearrange("p (u j) -> p u j", u=4), res_sb[1][:, :, js], ADD)
             nc.sync.dma_start(out[:, W + P * s : W + P * (s + 1)].rearrange("(u p) j -> p u j", p=P), o[:])
 
+        load_w1_scales()
+        gather_scales(1, 0)
         gather_scales(0, 0)
-        order_scales(0)
-        load_w2(0, 0)
-        gather_words(0, 0)
-        load_w2(0, 1)
         order_w0(0)
+        order_scales(0)
+        gather_words(0, 0)
+        gather_scales(2, 0)
+        cast_w2(0, 1)
+        gather_words(1, 0)
+        gather_words(2, 0)
+        gather_scales(0, 1)
         order_w0(1)
-        load_w2(1, 0)
+        order_w1(0)
+        cast_w2(0, 0)
         wide(0, 0, 0)
         wide(0, 1, 0)
-        gather_scales(1, 0)
-        order_scales(1)
-        gather_words(1, 0)
-        load_w2(1, 1)
-        order_w1(0)
         order_w1(1)
-        load_wd()
-        gather_scales(2, 0)
+        order_scales(1)
         wide(1, 0, 0)
-        wide(1, 1, 0)
-        gather_words(2, 0)
-        cast_w2(0, 0)
-        cast_w2(0, 1)
-        load_res(0)
-        quant_w2(0, 0)
         quant_w2(0, 1)
-        wide(2, 0, 0)
-        gather_scales(0, 1)
-        gather_words(0, 1)
         cast_w2(1, 0)
-        drain(0, 0)
-        cast_w2(1, 1)
-        load_res(1)
-        wide(0, 0, 1)
-        quant_w2(1, 0)
-        quant_w2(1, 1)
         gather_scales(1, 1)
+        wide(1, 1, 0)
+        gather_words(0, 1)
+        quant_w2(0, 0)
+        load_res(1)
+        wide(2, 0, 0)
+        cast_w2(1, 1)
+        gather_scales(2, 1)
+        quant_w2(1, 1)
+        quant_w2(1, 0)
+        drain(0, 0)
+        wide(0, 0, 1)
+        load_wd()
         gather_words(1, 1)
         wide(2, 1, 0)
-        drain(1, 0)
-        gather_scales(2, 1)
         gather_words(2, 1)
+        drain(1, 0)
+        weave(0, 0)
+        load_res(0)
         wide(1, 0, 1)
+        quant_h(0, 0)
+        narrow(0)
+        weave(1, 0)
+        narrow(2)
         wide(2, 0, 1)
         drain(0, 1)
-        weave(0, 0)
-        weave(1, 0)
-        quant_h(0, 0)
         quant_h(1, 0)
-        narrow(0)
-        weave(0, 1)
+        narrow(1)
+        second_wide(2)
+        weave(0, 1, nc.scalar.copy)
         quant_h(0, 1)
-        for u in range(4):
-            second_wide(u)
-        for s in range(1, 4):
-            narrow(s)
-            second_narrow(s - 1)
+        second_wide(3)
+        narrow(3)
+        second_wide(0)
+        second_narrow(1)
+        second_narrow(2)
+        second_wide(1)
+        second_narrow(0)
         second_narrow(3)

@@ -17,23 +17,32 @@ RELU = mybir.ActivationFunctionType.Relu
 ADD = mybir.AluOpType.add
 
 REUSES = {
-    "w1_sc_raw": "w0_raw0",
-    "wd_sc": "w0_raw0",
-    "both10": "w0_raw1",
-    "both20": "w1_raw0",
-    "tab_lo01": "w1_raw1",
-    "both01": "w2_bf01",
-    "both11": "w2_bf11",
-    "tab_lo21": "w2_bf10",
-    "both21": "w2_bf11",
-    "h_wv10": "w2_bf01",
-    "res0": "both10",
-    "h_wv00": "w2_bf11",
-    "h_pl10": "both21",
-    "res1": "w2_raw111"
+    "w2_raw02": "w2_bf11",
+    "both21": "w2_bf10",
+    "tab_lo21": "w1_raw1",
+    "both11": "w1_raw1",
+    "tab_lo11": "w2_raw13",
+    "w1_sc_raw": "w2_raw13",
+    "both20": "w2_raw13",
+    "w1_raw0": "w1_raw1",
+    "w1_raw1": "w2_bf11",
+    "h_pl00": "both20",
+    "w2_raw10": "w2_bf10",
+    "wd": "both20",
+    "w2_raw00": "w1_sc_raw",
+    "both10": "h_pl00",
+    "h_pl10": "w1_sc_raw",
+    "res0": "both11",
+    "w2_raw12": "h_pl00",
+    "both01": "w2_raw12",
+    "wd_sc": "both10",
+    "h_wv10": "w2_raw10",
+    "h_wv00": "w0_sc_raw",
+    "w0_raw1": "both10"
 }
 P = 128
 W = 512
+H = 256
 
 
 def tile_list_rvq_relu_res_kernel(
@@ -77,25 +86,30 @@ def tile_list_rvq_relu_res_kernel(
         late = {}
         res_sb = {}
 
-        def load_w0(b, eng=nc.sync):
-            w0_raw[b] = held([P, 2, W // 2], I32, "w0_raw%d" % b)
-            eng.dma_start(w0_raw[b][:], w0_words.rearrange("a p c -> p a c")[:, :, 2 * W * b : 2 * W * (b + 1)].bitcast(I32))
+        def load_w0(halves, eng=nc.sync):
+            raw = held([P, 2, W // 2 * len(halves)], I32, "w0_raw%d" % halves[0])
+            src = w0_words.rearrange("a p c -> p a c")[:, :, 2 * W * halves[0] : 2 * W * (halves[-1] + 1)]
+            eng.dma_start(raw[:], src.bitcast(I32))
+            for n, b in enumerate(halves):
+                w0_raw[b] = raw[:, :, W // 2 * n : W // 2 * (n + 1)]
 
-        def load_w1(b):
-            w1_raw[b] = held([P, 2, W], I32, "w1_raw%d" % b)
-            nc.sync.dma_start(
-                w1_raw[b][:], w1_words.rearrange("a p r i -> p a (r i)")[:, :, 4 * W * b : 4 * W * (b + 1)].bitcast(I32)
-            )
+        def load_w1(halves):
+            raw = held([P, 2, W * len(halves)], I32, "w1_raw%d" % halves[0])
+            src = w1_words.rearrange("a p r i -> p a (r i)")[:, :, 4 * W * halves[0] : 4 * W * (halves[-1] + 1)]
+            nc.sync.dma_start(raw[:], src.bitcast(I32))
+            for n, b in enumerate(halves):
+                w1_raw[b] = raw[:, :, W * n : W * (n + 1)]
 
         def load_w1_scales():
             raw_sc[1] = held([P, R], U8, "w1_sc_raw")
             nc.vector.memset(raw_sc[1][:].bitcast(I32), 0)
             load_scales(nc.scalar, raw_sc[1], w1_scales)
 
-        def load_w2(b, a, h):
-            w2_raw[b, a, h] = held([P, 4, W // 2], F32, "w2_raw%d%d%d" % (b, a, h))
-            c0 = W * b + W // 2 * h
-            nc.sync.dma_start(w2_raw[b, a, h][:], w2[W * a : W * (a + 1), c0 : c0 + W // 2].rearrange("(p i) c -> p i c", i=4))
+        def load_w2(a, q0, q1):
+            raw = held([P, 4, H * (q1 - q0)], F32, "w2_raw%d%d" % (a, q0))
+            nc.sync.dma_start(raw[:], w2[W * a : W * (a + 1), H * q0 : H * q1].rearrange("(p i) c -> p i c", i=4))
+            for q in range(q0, q1):
+                w2_raw[a, q] = raw[:, :, H * (q - q0) : H * (q - q0 + 1)]
 
         def load_wd():
             late["wd"] = held([P, 2, N], I32, "wd")
@@ -105,9 +119,10 @@ def tile_list_rvq_relu_res_kernel(
                 nc.sync.dma_start(late["wd_sc"][32 * q : 32 * q + 8, :].bitcast(I32), wd_scales[:, 4 * q : 4 * q + 4, :].bitcast(I32))
             nc.sync.dma_start(late["wd"][:], wd_words.rearrange("a p n i -> p a (n i)").bitcast(I32))
 
-        def load_res(c):
-            res_sb[c] = held([P, 4, W], F32, "res%d" % c)
-            nc.sync.dma_start(res_sb[c][:], res[:, W * c : W * (c + 1)].rearrange("(u p) j -> p u j", p=P))
+        def load_res(v):
+            raw = held([P, 2, J], F32, "res%d" % v)
+            nc.sync.dma_start(raw[:], res[2 * P * v : 2 * P * (v + 1), :].rearrange("(u p) j -> p u j", p=P))
+            res_sb[v] = raw
 
         tw = held([P, T], I32, "tw")
 
@@ -116,21 +131,11 @@ def tile_list_rvq_relu_res_kernel(
 
         load_scales(nc.scalar, tsc, tab_scales, (2, 3))
         load_scales(nc.scalar, raw_sc[0], w0_scales)
+        load_w0([0])
         warm_up()
+        load_w0([1])
         load_scales(nc.sync, tsc, tab_scales, (0, 1))
-        load_w0(0)
         load_tw(nc.sync)
-        load_w2(0, 0, 0)
-        load_w0(1)
-        load_w1(0)
-        load_w2(0, 1, 0)
-        load_w2(1, 0, 0)
-        load_w2(0, 0, 1)
-        load_w1(1)
-        load_w2(0, 1, 1)
-        load_w2(1, 0, 1)
-        load_w2(1, 1, 0)
-        load_w2(1, 1, 1)
         tab_lo = {}
         tab_x = {}
         w_lo = {}
@@ -182,31 +187,31 @@ def tile_list_rvq_relu_res_kernel(
             w_x[0, b] = held([P, 2, 2 * W], U8, "w0_x%d" % b)
             nc.vector.tensor_copy(
                 w_x[0, b][:].bitcast(U16).rearrange("p a (t m) -> p a t m", t=4),
-                w0_raw[b][:].bitcast(U16).rearrange("p a (m t) -> p a t m", t=4),
+                w0_raw[b].bitcast(U16).rearrange("p a (m t) -> p a t m", t=4),
             )
 
         def order_w1(b):
             w_x[1, b] = held([P, 2, W], I32, "w1_x%d" % b)
             nc.vector.tensor_copy(
-                w_x[1, b][:].rearrange("p a (t m) -> p a m t", t=4), w1_raw[b][:].rearrange("p a (m t) -> p a m t", t=4)
+                w_x[1, b][:].rearrange("p a (t m) -> p a m t", t=4), w1_raw[b].rearrange("p a (m t) -> p a m t", t=4)
             )
 
         w2_bf = {}
 
-        def cast_w2(b, a):
-            w2_bf[b, a] = held([P, 4 * W], BF16, "w2_bf%d%d" % (b, a))
-            for h in range(2):
-                nc.scalar.copy(
-                    w2_bf[b, a][:].rearrange("p (t m i) -> p m i t", t=4, i=4)[:, 64 * h : 64 * (h + 1)],
-                    w2_raw[b, a, h][:].rearrange("p i (m t) -> p m i t", t=4),
-                )
+        def cast_w2(b, a, h):
+            if (b, a) not in w2_bf:
+                w2_bf[b, a] = held([P, 4 * W], BF16, "w2_bf%d%d" % (b, a))
+            nc.scalar.copy(
+                w2_bf[b, a][:].rearrange("p (t m i) -> p m i t", t=4, i=4)[:, 64 * h : 64 * (h + 1)],
+                w2_raw[a, 2 * b + h].rearrange("p i (m t) -> p m i t", t=4),
+            )
 
         def quant_w2(b, a):
             w_x[2, b, a] = held([P, W], U32, "w2_x%d%d" % (b, a))
             w2_sc[b, a] = held([P, W], U8, "w2_sc%d%d" % (b, a))
             nc.vector.quantize_mx(out=w_x[2, b, a][:].bitcast(FP8X4), scales=w2_sc[b, a][:], in_=w2_bf[b, a][:])
 
-        def mm1(dst, g, a, b, t, c, j0, n):
+        def mm1(dst, g, a, b, t, c, j0, n, start, stop):
             m = slice(P * t, P * (t + 1))
             if g == 0:
                 lhs = w_x[0, b][:, a, 2 * P * t : 2 * P * (t + 1)].bitcast(FP4X4)
@@ -225,19 +230,19 @@ def tile_list_rvq_relu_res_kernel(
                 lhsT_scale=lhs_sc,
                 rhs=tab_x[g, c][:, a, 2 * j0 : 2 * (j0 + n)].bitcast(FP4X4),
                 rhs_scale=rhs_sc,
-                start=(g == 0 and a == 0),
-                stop=(g == 2 and a == 1),
+                start=start,
+                stop=stop,
             )
 
-        def wide(g, b, c):
-            if g == 0:
+        passes_done = {}
+
+        def wide(g, a, b, c):
+            done = passes_done.get((b, c), 0)
+            passes_done[b, c] = done + 1
+            if done == 0:
                 banks[b, c] = [psum.tile([P, W], F32, name="bank") for t in range(4)]
-            if g < 2:
-                order = [(a, t) for a in range(2) for t in range(4)]
-            else:
-                order = [(0, t) for t in range(2)] + [(1, 0), (0, 2), (1, 1), (0, 3), (1, 2), (1, 3)]
-            for a, t in order:
-                mm1(banks[b, c][t][:], g, a, b, t, c, 0, W)
+            for t in range(4):
+                mm1(banks[b, c][t][:], g, a, b, t, c, 0, W, done == 0, done == 5)
 
         planes = {}
 
@@ -271,95 +276,118 @@ def tile_list_rvq_relu_res_kernel(
                 stop=(b == 1),
             )
 
-        def second_wide(u):
-            bank = psum.tile([P, W], F32, name="bank")
-            for b in range(2):
-                mm2(bank[:], u, b, h_x[b, 0][:], h_sc[b, 0][:])
-            o = held([P, W], F32, "o_wide%d" % u)
-            nc.vector.tensor_tensor(o[:], bank[:], res_sb[0][:, u, :], ADD)
-            nc.sync.dma_start(out[P * u : P * (u + 1), 0:W], o[:])
-
         def narrow(s):
             bank = psum.tile([P, W], F32, name="bank")
             for t in range(4):
                 for g in range(3):
                     for a in range(2):
-                        mm1(bank[:, P * t : P * (t + 1)], g, a, 1, t, 1, P * s, P)
+                        mm1(bank[:, P * t : P * (t + 1)], g, a, 1, t, 1, P * s, P, g + a == 0, g + a == 3)
             wv = held([P, W], BF16, "h_nw%d" % s)
             nc.scalar.activation(
                 wv[:].rearrange("p (j t) -> p j t", t=4), bank[:].rearrange("p (t j) -> p j t", t=4), RELU
             )
-            h_x[1, 1, s] = held([P, P], U32, "h_nx%d" % s)
-            h_sc[1, 1, s] = held([P, P], U8, "h_nsc%d" % s)
-            nc.vector.quantize_mx(out=h_x[1, 1, s][:].bitcast(FP8X4), scales=h_sc[1, 1, s][:], in_=wv[:])
-
-        def second_narrow(s):
-            bank = psum.tile([P, W], F32, name="bank")
+            if (1, 1) not in h_x:
+                h_x[1, 1] = held([P, W], U32, "h_x11")
+                h_sc[1, 1] = held([P, W], U8, "h_sc11")
             js = slice(P * s, P * (s + 1))
-            for u in range(4):
-                mm2(bank[:, P * u : P * (u + 1)], u, 0, h_x[0, 1][:, js], h_sc[0, 1][:, js])
-                mm2(bank[:, P * u : P * (u + 1)], u, 1, h_x[1, 1, s][:], h_sc[1, 1, s][:])
-            o = held([P, 4, P], F32, "o_nw%d" % s)
-            nc.vector.tensor_tensor(o[:], bank[:].rearrange("p (u j) -> p u j", u=4), res_sb[1][:, :, js], ADD)
-            nc.sync.dma_start(out[:, W + P * s : W + P * (s + 1)].rearrange("(u p) j -> p u j", p=P), o[:])
+            nc.vector.quantize_mx(out=h_x[1, 1][:, js].bitcast(FP8X4), scales=h_sc[1, 1][:, js], in_=wv[:])
 
+        def second(c, j0, n, u0):
+            count = W // n
+            bank = psum.tile([P, W], F32, name="bank")
+            js = slice(j0, j0 + n)
+            for x in range(count):
+                for b in range(2):
+                    mm2(bank[:, n * x : n * (x + 1)], u0 + x, b, h_x[b, c][:, js], h_sc[b, c][:, js])
+            o = held([P, count, n], F32, "o%d%d%d" % (c, j0 // P, u0))
+            cols = slice(W * c + j0, W * c + j0 + n)
+            for x0 in range(0, count, 2):
+                x1 = min(count, x0 + 2)
+                u = u0 + x0
+                nc.vector.tensor_tensor(
+                    o[:, x0:x1, :],
+                    bank[:].rearrange("p (u j) -> p u j", j=n)[:, x0:x1, :],
+                    res_sb[u // 2][:, u % 2 : u % 2 + x1 - x0, cols],
+                    ADD,
+                )
+            nc.sync.dma_start(out[P * u0 : P * (u0 + count), cols].rearrange("(u p) j -> p u j", p=P), o[:])
+
+        load_w1([1])
         load_w1_scales()
-        gather_scales(1, 0)
-        gather_scales(0, 0)
         order_w0(0)
+        load_w2(1, 0, 2)
         order_scales(0)
-        gather_words(0, 0)
-        gather_scales(2, 0)
-        cast_w2(0, 1)
-        gather_words(1, 0)
-        gather_words(2, 0)
-        gather_scales(0, 1)
-        order_w0(1)
-        order_w1(0)
-        cast_w2(0, 0)
-        wide(0, 0, 0)
-        wide(0, 1, 0)
-        order_w1(1)
         order_scales(1)
-        wide(1, 0, 0)
+        cast_w2(0, 1, 1)
+        gather_words(2, 0)
+        load_w2(0, 0, 2)
+        cast_w2(0, 0, 1)
+        gather_words(0, 0)
+        gather_scales(0, 1)
+        load_w1([0])
+        gather_scales(1, 0)
+        cast_w2(0, 0, 0)
+        gather_scales(0, 0)
+        order_w0(1)
+        wide(0, 0, 0, 0)
+        gather_scales(2, 0)
+        cast_w2(0, 1, 0)
+        order_w1(0)
+        wide(0, 0, 1, 0)
+        gather_words(1, 0)
+        wide(0, 1, 1, 0)
+        load_w2(0, 2, 4)
         quant_w2(0, 1)
-        cast_w2(1, 0)
-        gather_scales(1, 1)
-        wide(1, 1, 0)
-        gather_words(0, 1)
         quant_w2(0, 0)
+        order_w1(1)
+        wide(0, 1, 0, 0)
+        gather_words(0, 1)
+        cast_w2(1, 0, 1)
         load_res(1)
-        wide(2, 0, 0)
-        cast_w2(1, 1)
-        gather_scales(2, 1)
-        quant_w2(1, 1)
-        quant_w2(1, 0)
-        drain(0, 0)
-        wide(0, 0, 1)
-        load_wd()
+        load_w2(1, 2, 4)
+        wide(1, 0, 0, 0)
+        wide(1, 0, 1, 0)
+        wide(0, 0, 0, 1)
+        wide(1, 1, 0, 0)
+        cast_w2(1, 1, 0)
+        wide(2, 0, 0, 0)
+        gather_scales(1, 1)
         gather_words(1, 1)
-        wide(2, 1, 0)
+        wide(2, 1, 0, 0)
+        gather_scales(2, 1)
         gather_words(2, 1)
-        drain(1, 0)
-        weave(0, 0)
+        cast_w2(1, 0, 0)
         load_res(0)
-        wide(1, 0, 1)
+        quant_w2(1, 0)
+        wide(1, 1, 1, 0)
+        cast_w2(1, 1, 1)
+        wide(0, 1, 0, 1)
+        wide(2, 0, 1, 0)
+        quant_w2(1, 1)
+        wide(1, 0, 0, 1)
+        drain(0, 0)
+        wide(2, 1, 1, 0)
+        weave(0, 0)
+        wide(1, 1, 0, 1)
+        wide(2, 0, 0, 1)
+        wide(2, 1, 0, 1)
+        drain(1, 0)
+        drain(0, 1)
+        weave(0, 1)
         quant_h(0, 0)
         narrow(0)
-        weave(1, 0)
-        narrow(2)
-        wide(2, 0, 1)
-        drain(0, 1)
-        quant_h(1, 0)
-        narrow(1)
-        second_wide(2)
-        weave(0, 1, nc.scalar.copy)
-        quant_h(0, 1)
-        second_wide(3)
         narrow(3)
-        second_wide(0)
-        second_narrow(1)
-        second_narrow(2)
-        second_wide(1)
-        second_narrow(0)
-        second_narrow(3)
+        narrow(2)
+        quant_h(0, 1)
+        weave(1, 0)
+        load_wd()
+        quant_h(1, 0)
+        second(0, 0, 512, 3)
+        second(1, 256, 256, 0)
+        second(0, 0, 512, 2)
+        narrow(1)
+        second(0, 0, 512, 0)
+        second(1, 256, 256, 2)
+        second(1, 0, 256, 0)
+        second(0, 0, 512, 1)
+        second(1, 0, 256, 2)

from contextlib import ExitStack

import concourse.mybir as mybir

K, R, N, T, J = 1024, 1024, 512, 4096, 1024
FLOPS = 2 * (3 * K * R * J + R * N * J)

F32 = mybir.dt.float32
BF16 = mybir.dt.bfloat16
I32 = mybir.dt.int32
U32 = mybir.dt.uint32
U16 = mybir.dt.uint16
U8 = mybir.dt.uint8
FP8X4 = mybir.dt.float8_e4m3fn_x4
FP4X4 = mybir.dt.float4_e2m1fn_x4
RELU = mybir.ActivationFunctionType.Relu
ADD = mybir.AluOpType.add

REUSES = {
    "w2_raw02": "w2_bf11",
    "both21": "w2_bf10",
    "tab_lo21": "w1_raw1",
    "both11": "w1_raw1",
    "tab_lo11": "w2_raw13",
    "w1_sc_raw": "w2_raw13",
    "both20": "w2_raw13",
    "w1_raw0": "w1_raw1",
    "w1_raw1": "w2_bf11",
    "h_pl00": "both20",
    "w2_raw10": "w2_bf10",
    "wd": "both20",
    "w2_raw00": "w1_sc_raw",
    "both10": "h_pl00",
    "h_pl10": "w1_sc_raw",
    "res0": "both11",
    "w2_raw12": "h_pl00",
    "both01": "w2_raw12",
    "wd_sc": "both10",
    "h_wv10": "w2_raw10",
    "h_wv00": "w0_sc_raw",
    "w0_raw1": "both10"
}
P = 128
W = 512
H = 256


def tile_list_rvq_relu_res_kernel(
    tc, tab_words, tab_scales, w0_words, w0_scales, w1_words, w1_scales, w2, wd_words, wd_scales, res, offs, out
):
    nc = tc.nc
    with ExitStack() as ctx:
        keep = ctx.enter_context(tc.tile_pool(name="keep", bufs=1))
        psum = ctx.enter_context(tc.psum_pool(name="psum", bufs=8))

        def held(shape, dtype, name):
            return keep.tile(shape, dtype, name=name, tag=REUSES.get(name, name), align_bytes=64)

        offsets = keep.tile([P, 3 * J // 16], U16, name="offsets")
        nc.sync.dma_start(offsets[:], offs)

        raw_sc = {0: held([P, R], U8, "w0_sc_raw")}
        up_sc = [held([P, R], U8, "w0_sc_up"), held([P, R], U8, "w1_sc_up")]
        tab_up = held([P, 6, W], U8, "tab_up")
        tsc = held([P, T], U8, "tsc")
        nc.vector.memset(tsc[:, 0 : T // 2].bitcast(I32), 0)
        nc.gpsimd.memset(tsc[:, T // 2 : T].bitcast(I32), 0)
        for t_ in (raw_sc[0], up_sc[0], up_sc[1]):
            nc.vector.memset(t_[:].bitcast(I32), 0)
        nc.vector.memset(tab_up[:].rearrange("p a w -> p (a w)").bitcast(I32), 0)


        def warm_up():
            warm = held([P, 16], BF16, "warm")
            nc.scalar.activation(warm[:], up_sc[0][:, 0:32].bitcast(BF16), RELU)


        def load_scales(eng, tile_, src, which=range(4)):
            rows = src.rearrange("a (q r) t -> r q a t", r=4)
            for r in which:
                eng.dma_start(tile_[r:P:16, :].bitcast(I32), rows[r].bitcast(I32))

        w0_raw = {}
        w1_raw = {}
        w2_raw = {}
        late = {}
        res_sb = {}

        def load_w0(halves, eng=nc.sync):
            raw = held([P, 2, W // 2 * len(halves)], I32, "w0_raw%d" % halves[0])
            src = w0_words.rearrange("a p c -> p a c")[:, :, 2 * W * halves[0] : 2 * W * (halves[-1] + 1)]
            eng.dma_start(raw[:], src.bitcast(I32))
            for n, b in enumerate(halves):
                w0_raw[b] = raw[:, :, W // 2 * n : W // 2 * (n + 1)]

        def load_w1(halves):
            raw = held([P, 2, W * len(halves)], I32, "w1_raw%d" % halves[0])
            src = w1_words.rearrange("a p r i -> p a (r i)")[:, :, 4 * W * halves[0] : 4 * W * (halves[-1] + 1)]
            nc.sync.dma_start(raw[:], src.bitcast(I32))
            for n, b in enumerate(halves):
                w1_raw[b] = raw[:, :, W * n : W * (n + 1)]

        def load_w1_scales():
            raw_sc[1] = held([P, R], U8, "w1_sc_raw")
            nc.vector.memset(raw_sc[1][:].bitcast(I32), 0)
            load_scales(nc.scalar, raw_sc[1], w1_scales)

        def load_w2(a, q0, q1):
            raw = held([P, 4, H * (q1 - q0)], F32, "w2_raw%d%d" % (a, q0))
            nc.sync.dma_start(raw[:], w2[W * a : W * (a + 1), H * q0 : H * q1].rearrange("(p i) c -> p i c", i=4))
            for q in range(q0, q1):
                w2_raw[a, q] = raw[:, :, H * (q - q0) : H * (q - q0 + 1)]

        def load_wd():
            late["wd"] = held([P, 2, N], I32, "wd")
            late["wd_sc"] = held([P, N], U8, "wd_sc")
            nc.vector.memset(late["wd_sc"][:].bitcast(I32), 0)
            for q in range(4):
                nc.sync.dma_start(late["wd_sc"][32 * q : 32 * q + 8, :].bitcast(I32), wd_scales[:, 4 * q : 4 * q + 4, :].bitcast(I32))
            nc.sync.dma_start(late["wd"][:], wd_words.rearrange("a p n i -> p a (n i)").bitcast(I32))

        def load_res(v):
            raw = held([P, 2, J], F32, "res%d" % v)
            nc.sync.dma_start(raw[:], res[2 * P * v : 2 * P * (v + 1), :].rearrange("(u p) j -> p u j", p=P))
            res_sb[v] = raw

        tw = held([P, T], I32, "tw")

        def load_tw(eng):
            eng.dma_start(tw[:], tab_words[0].rearrange("p t i -> p (t i)").bitcast(I32))

        load_scales(nc.scalar, tsc, tab_scales, (2, 3))
        load_scales(nc.scalar, raw_sc[0], w0_scales)
        load_w0([0])
        warm_up()
        load_w0([1])
        load_scales(nc.sync, tsc, tab_scales, (0, 1))
        load_tw(nc.sync)
        tab_lo = {}
        tab_x = {}
        w_lo = {}
        w_x = {}
        w2_sc = {}
        h_x = {}
        h_sc = {}
        banks = {}

        def piece(g, c):
            k0 = (g * J + c * W) // 16
            return offsets[:, k0 : k0 + W // 16]

        first_lo = held([P, 3, W], U8, "first_lo")

        def gather_scales(g, c):
            if c == 0:
                tab_lo[g, c] = first_lo[:, g, :]
            else:
                tab_lo[g, c] = held([P, W], U8, "tab_lo%d%d" % (g, c))[:]
            nc.vector.tensor_copy(tab_lo[g, c], tsc[:].indirect(piece(g, c)))
            if c == 1:
                nc.sync.dma_start(tab_up[0:112, 3 + g, :].bitcast(I32), tab_lo[g, c][16:128, :].bitcast(I32))
            elif g == 2:
                nc.scalar.dma_start(
                    tab_up[0:112, 0:3, :].rearrange("p g w -> p (g w)").bitcast(I32),
                    first_lo[16:128].rearrange("p g w -> p (g w)").bitcast(I32),
                )

        def gather_words(g, c):
            both = held([P, W], U32, "both%d%d" % (g, c))
            nc.vector.tensor_copy(both[:], tw[:].bitcast(U32).indirect(piece(g, c)))
            tab_x[g, c] = held([P, 2, 2 * W], U8, "tab_x%d%d" % (g, c))
            halves = both[:].bitcast(U16).rearrange("p (j d) -> p d j", d=2)
            if (g, c) == (0, 0):
                for a in range(2):
                    nc.vector.tensor_copy(tab_x[g, c][:, a, :].bitcast(U16), halves[:, a, :])
            else:
                nc.vector.tensor_copy(tab_x[g, c][:].bitcast(U16), halves)

        def order_scales(g):
            w_lo[g] = held([P, R], U8, "w_lo%d" % g)
            nc.vector.tensor_copy(
                w_lo[g][:].rearrange("p (b t m) -> p b t m", b=2, t=4), raw_sc[g][:].rearrange("p (b m t) -> p b t m", b=2, t=4)
            )
            nc.scalar.dma_start(up_sc[g][0:112, :].bitcast(I32), w_lo[g][16:128, :].bitcast(I32))

        def order_w0(b):
            w_x[0, b] = held([P, 2, 2 * W], U8, "w0_x%d" % b)
            nc.vector.tensor_copy(
                w_x[0, b][:].bitcast(U16).rearrange("p a (t m) -> p a t m", t=4),
                w0_raw[b].bitcast(U16).rearrange("p a (m t) -> p a t m", t=4),
            )

        def order_w1(b):
            w_x[1, b] = held([P, 2, W], I32, "w1_x%d" % b)
            nc.vector.tensor_copy(
                w_x[1, b][:].rearrange("p a (t m) -> p a m t", t=4), w1_raw[b].rearrange("p a (m t) -> p a m t", t=4)
            )

        w2_bf = {}

        def cast_w2(b, a, h):
            if (b, a) not in w2_bf:
                w2_bf[b, a] = held([P, 4 * W], BF16, "w2_bf%d%d" % (b, a))
            nc.scalar.copy(
                w2_bf[b, a][:].rearrange("p (t m i) -> p m i t", t=4, i=4)[:, 64 * h : 64 * (h + 1)],
                w2_raw[a, 2 * b + h].rearrange("p i (m t) -> p m i t", t=4),
            )

        def quant_w2(b, a):
            w_x[2, b, a] = held([P, W], U32, "w2_x%d%d" % (b, a))
            w2_sc[b, a] = held([P, W], U8, "w2_sc%d%d" % (b, a))
            nc.vector.quantize_mx(out=w_x[2, b, a][:].bitcast(FP8X4), scales=w2_sc[b, a][:], in_=w2_bf[b, a][:])

        def mm1(dst, g, a, b, t, c, j0, n, start, stop):
            m = slice(P * t, P * (t + 1))
            if g == 0:
                lhs = w_x[0, b][:, a, 2 * P * t : 2 * P * (t + 1)].bitcast(FP4X4)
            elif g == 1:
                lhs = w_x[1, b][:, a, m].bitcast(FP8X4)
            else:
                lhs = w_x[2, b, a][:, m].bitcast(FP8X4)
            if g < 2:
                lhs_sc = (w_lo, up_sc)[a][g][:, W * b + P * t : W * b + P * (t + 1)]
            else:
                lhs_sc = w2_sc[b, a][:, m]
            rhs_sc = tab_lo[g, c][:, j0 : j0 + n] if a == 0 else tab_up[:, g + 3 * c, j0 : j0 + n]
            nc.tensor.matmul_mx(
                out=dst,
                lhsT=lhs,
                lhsT_scale=lhs_sc,
                rhs=tab_x[g, c][:, a, 2 * j0 : 2 * (j0 + n)].bitcast(FP4X4),
                rhs_scale=rhs_sc,
                start=start,
                stop=stop,
            )

        passes_done = {}

        def wide(g, a, b, c):
            done = passes_done.get((b, c), 0)
            passes_done[b, c] = done + 1
            if done == 0:
                banks[b, c] = [psum.tile([P, W], F32, name="bank") for t in range(4)]
            for t in range(4):
                mm1(banks[b, c][t][:], g, a, b, t, c, 0, W, done == 0, done == 5)

        planes = {}

        def drain(b, c):
            planes[b, c] = held([P, 4, W], BF16, "h_pl%d%d" % (b, c))
            for t in range(4):
                nc.scalar.activation(planes[b, c][:, t, :], banks[b, c][t][:], RELU)

        woven = {}

        def weave(b, c, copy=nc.vector.tensor_copy):
            woven[b, c] = held([P, 4 * W], BF16, "h_wv%d%d" % (b, c))
            copy(
                woven[b, c][:].rearrange("p (c i t) -> p c t i", i=4, t=4),
                planes[b, c][:].rearrange("p t (c i) -> p c t i", i=4),
            )

        def quant_h(b, c):
            h_x[b, c] = held([P, W], U32, "h_x%d%d" % (b, c))
            h_sc[b, c] = held([P, W], U8, "h_sc%d%d" % (b, c))
            nc.vector.quantize_mx(out=h_x[b, c][:].bitcast(FP8X4), scales=h_sc[b, c][:], in_=woven[b, c][:])

        def mm2(dst, u, b, x, sc):
            nc.tensor.matmul_mx(
                out=dst,
                lhsT=late["wd"][:, b, P * u : P * (u + 1)].bitcast(FP8X4),
                lhsT_scale=late["wd_sc"][4 * b :, P * u : P * (u + 1)],
                rhs=x.bitcast(FP8X4),
                rhs_scale=sc,
                start=(b == 0),
                stop=(b == 1),
            )

        def narrow(s):
            bank = psum.tile([P, W], F32, name="bank")
            for t in range(4):
                for g in range(3):
                    for a in range(2):
                        mm1(bank[:, P * t : P * (t + 1)], g, a, 1, t, 1, P * s, P, g + a == 0, g + a == 3)
            wv = held([P, W], BF16, "h_nw%d" % s)
            nc.scalar.activation(
                wv[:].rearrange("p (j t) -> p j t", t=4), bank[:].rearrange("p (t j) -> p j t", t=4), RELU
            )
            if (1, 1) not in h_x:
                h_x[1, 1] = held([P, W], U32, "h_x11")
                h_sc[1, 1] = held([P, W], U8, "h_sc11")
            js = slice(P * s, P * (s + 1))
            nc.vector.quantize_mx(out=h_x[1, 1][:, js].bitcast(FP8X4), scales=h_sc[1, 1][:, js], in_=wv[:])

        def second(c, j0, n, u0):
            count = W // n
            bank = psum.tile([P, W], F32, name="bank")
            js = slice(j0, j0 + n)
            for x in range(count):
                for b in range(2):
                    mm2(bank[:, n * x : n * (x + 1)], u0 + x, b, h_x[b, c][:, js], h_sc[b, c][:, js])
            o = held([P, count, n], F32, "o%d%d%d" % (c, j0 // P, u0))
            cols = slice(W * c + j0, W * c + j0 + n)
            for x0 in range(0, count, 2):
                x1 = min(count, x0 + 2)
                u = u0 + x0
                nc.vector.tensor_tensor(
                    o[:, x0:x1, :],
                    bank[:].rearrange("p (u j) -> p u j", j=n)[:, x0:x1, :],
                    res_sb[u // 2][:, u % 2 : u % 2 + x1 - x0, cols],
                    ADD,
                )
            nc.sync.dma_start(out[P * u0 : P * (u0 + count), cols].rearrange("(u p) j -> p u j", p=P), o[:])

        load_w1([1])
        load_w1_scales()
        order_w0(0)
        load_w2(1, 0, 2)
        order_scales(0)
        order_scales(1)
        cast_w2(0, 1, 1)
        gather_words(2, 0)
        load_w2(0, 0, 2)
        cast_w2(0, 0, 1)
        gather_words(0, 0)
        gather_scales(0, 1)
        load_w1([0])
        gather_scales(1, 0)
        cast_w2(0, 0, 0)
        gather_scales(0, 0)
        order_w0(1)
        wide(0, 0, 0, 0)
        gather_scales(2, 0)
        cast_w2(0, 1, 0)
        order_w1(0)
        wide(0, 0, 1, 0)
        gather_words(1, 0)
        wide(0, 1, 1, 0)
        load_w2(0, 2, 4)
        quant_w2(0, 1)
        quant_w2(0, 0)
        order_w1(1)
        wide(0, 1, 0, 0)
        gather_words(0, 1)
        cast_w2(1, 0, 1)
        load_res(1)
        load_w2(1, 2, 4)
        wide(1, 0, 0, 0)
        wide(1, 0, 1, 0)
        wide(0, 0, 0, 1)
        wide(1, 1, 0, 0)
        cast_w2(1, 1, 0)
        wide(2, 0, 0, 0)
        gather_scales(1, 1)
        gather_words(1, 1)
        wide(2, 1, 0, 0)
        gather_scales(2, 1)
        gather_words(2, 1)
        cast_w2(1, 0, 0)
        load_res(0)
        quant_w2(1, 0)
        wide(1, 1, 1, 0)
        cast_w2(1, 1, 1)
        wide(0, 1, 0, 1)
        wide(2, 0, 1, 0)
        quant_w2(1, 1)
        wide(1, 0, 0, 1)
        drain(0, 0)
        wide(2, 1, 1, 0)
        weave(0, 0)
        wide(1, 1, 0, 1)
        wide(2, 0, 0, 1)
        wide(2, 1, 0, 1)
        drain(1, 0)
        drain(0, 1)
        weave(0, 1)
        quant_h(0, 0)
        narrow(0)
        narrow(3)
        narrow(2)
        quant_h(0, 1)
        weave(1, 0)
        load_wd()
        quant_h(1, 0)
        second(0, 0, 512, 3)
        second(1, 256, 256, 0)
        second(0, 0, 512, 2)
        narrow(1)
        second(0, 0, 512, 0)
        second(1, 256, 256, 2)
        second(1, 0, 256, 0)
        second(0, 0, 512, 1)
        second(1, 0, 256, 2)
